import numpy as np
import ml_dtypes


def mxq(x, axis, fmt="e4m3"):
    dtype, down = {"e4m3": (ml_dtypes.float8_e4m3fn, 7), "e5m2": (ml_dtypes.float8_e5m2, 14)}[fmt]
    v = np.moveaxis(np.asarray(x, np.float32).astype(ml_dtypes.bfloat16).astype(np.float64), axis, -1)
    blocks = v.reshape(v.shape[:-1] + (-1, 32))
    amax = np.abs(blocks).max(-1, keepdims=True)
    byte = np.maximum(np.where(amax > 0, np.frexp(amax)[1] - 1 + 127, 0) - down, 1)
    scale = np.exp2(byte - 127.0)
    codes = (blocks / scale).astype(np.float32).astype(dtype).astype(np.float64)
    return np.moveaxis((codes * scale).reshape(v.shape), -1, axis)


WIDE = False


def mx_kscale(k):
    if not WIDE:
        return np.ones(k)
    levels = np.array([10, -10, 5, -5, 0])
    if k % 512:
        return np.exp2(np.random.permutation(np.resize(levels, k // 32))).repeat(32)
    a = np.empty((k // 512, 16))
    for p in range(k // 512):
        a[p, :8] = np.random.permutation(np.resize(levels, 8))
        for g in range(8):
            far = levels[np.abs(levels - a[p, g]) >= 10]
            a[p, g + 8] = far[np.random.randint(len(far))]
    return np.exp2(a.ravel()).repeat(32)


def f64(x):
    return np.asarray(x).astype(np.float64)


def striped(idx):
    return np.tile(idx.reshape(-1, 16).T, (8, 1)).astype(np.uint16)


def unstriped(offs):
    return offs[:16].T.reshape(-1).astype(np.int64)


def pack_weight(w):
    k, n = w.shape
    w = f64(np.asarray(w, np.float32).astype(ml_dtypes.bfloat16)).reshape(k // 32, 32, n)
    amax = np.abs(w).max(1)
    byte = np.clip(np.where(amax > 0, np.frexp(amax)[1] - 1 + 127 - 7, 1), 1, 254)
    scaled = (w * np.exp2(127.0 - byte)[:, None, :]).reshape(k, n).astype(np.float32)
    words = np.ascontiguousarray(scaled.reshape(k // 512, 128, 4, n).transpose(0, 1, 3, 2)).astype(ml_dtypes.float8_e4m3fn).view(np.uint8)
    return words, np.ascontiguousarray(byte.astype(np.uint8).reshape(k // 512, 16, n))


def unpack_weight(words, scales):
    g, p, n, _ = words.shape
    vals = np.ascontiguousarray(words).view(ml_dtypes.float8_e4m3fn).astype(np.float64) * np.repeat(np.exp2(scales.astype(np.float64) - 127.0), 8, axis=1)[..., None]
    return vals.transpose(0, 1, 3, 2).reshape(g * 512, n)


K, T, S, N, V = 512, 1024, 512, 128, 256
P = 2 ** 7


def setup_inputs():
    n = np.random.standard_normal
    s = mx_kscale(K)[:, None]
    packed_xT = pack_weight(n((K, T)) * s)
    return {
        "x_words": packed_xT[0],
        "x_scales": packed_xT[1],
        "w1": (n((K, N)) / np.sqrt(K) / s).astype(np.float32),
        "inv": (np.tile(np.random.uniform(0.3, 1.5, S), (P, 1))).astype(np.float32),
        "cnt": (np.tile(np.floor(np.random.uniform(1.0, 9.0, S)), (P, 1))).astype(np.float32),
        "offs": striped(np.random.permutation(T)[:S]),
        "pos1": striped(np.random.permutation(S)[:V]),
        "pos2": striped(np.random.permutation(S)[:V]),
        "pos3": striped(np.random.permutation(S)[:V]),
    }


def reference(x_words, x_scales, w1, inv, cnt, offs, pos1, pos2, pos3):
    xq = unpack_weight(x_words, x_scales)[:, unstriped(offs)]
    y = mxq(f64(w1), 0, "e4m3").T @ xq
    tgt = np.log(np.exp(y) + 1.0)
    res = tgt * (f64(inv)[:1] * f64(cnt)[:1])
    g0 = res[:, unstriped(pos1)]
    g1 = res[:, unstriped(pos2)]
    g2 = res[:, unstriped(pos3)]
    tot = g0 + g1 + g2
    pm = (g0 * tgt[:, unstriped(pos1)] + g1 * tgt[:, unstriped(pos2)] + g2 * tgt[:, unstriped(pos3)]) / tot
    return tot / (pm * (f64(cnt)[:1][:, unstriped(pos1)] + f64(cnt)[:1][:, unstriped(pos2)] + f64(cnt)[:1][:, unstriped(pos3)]) + 0.5)

@@ -1,0 +1,154 @@
+from contextlib import ExitStack
+
+import concourse.mybir as mybir
+
+K, T, S, N, V = 512, 1024, 512, 128, 256
+FLOPS = 2 * K * N * S
+
+F32 = mybir.dt.float32
+BF16 = mybir.dt.bfloat16
+I32 = mybir.dt.int32
+U32 = mybir.dt.uint32
+U16 = mybir.dt.uint16
+U8 = mybir.dt.uint8
+FP8X4 = mybir.dt.float8_e4m3fn_x4
+ALU = mybir.AluOpType
+ACT = mybir.ActivationFunctionType
+
+P = 128
+PACK = 4
+STRIPE = 16
+SOFTPLUS_CAP = 40.0
+TINY = 1e-30
+SAMPLE_CHUNKS = ((0, 256), (256, 512))
+LN_CUT = 272
+PIXEL_CHUNKS = ((0, 128), (128, 256))
+
+
+def tile_picked_yrestir_inv_p_kernel(
+    tc, x_words, x_scales, w1, inv, cnt, offs, pos1, pos2, pos3, out
+):
+    nc = tc.nc
+    with ExitStack() as ctx:
+        keep = ctx.enter_context(tc.tile_pool(name="keep", bufs=1))
+        psum = ctx.enter_context(tc.psum_pool(name="psum", bufs=1))
+
+        offs_sb = keep.tile([P, S // STRIPE], U16, name="offs_sb")
+        nc.sync.dma_start(offs_sb[:], offs)
+
+        scale_table = keep.tile([P, T], U8, name="scale_table", align_bytes=64)
+        nc.vector.memset(scale_table[:].bitcast(I32), 0)
+        for q in range(4):
+            nc.scalar.dma_start(
+                scale_table[32 * q : 32 * q + 4, :].bitcast(I32),
+                x_scales[0][4 * q : 4 * q + 4, :].bitcast(I32),
+            )
+
+        w_raw = keep.tile([P, PACK, N], F32, name="w_raw")
+        nc.sync.dma_start(w_raw[:], w1.rearrange("(p j) m -> p j m", j=PACK))
+        word_table = keep.tile([P, T], I32, name="word_table", align_bytes=64)
+        nc.sync.dma_start(word_table[:], x_words[0].rearrange("p n t -> p (n t)").bitcast(I32))
+        cnt_sb = keep.tile([P, S], F32, name="cnt_sb")
+        nc.sync.dma_start(cnt_sb[:], cnt)
+        pos_sb = []
+        for i, pos in enumerate((pos1, pos2, pos3)):
+            pos_tile = keep.tile([P, V // STRIPE], U16, name="pos_sb%d" % i)
+            nc.sync.dma_start(pos_tile[:], pos)
+            pos_sb.append(pos_tile)
+        inv_sb = keep.tile([P, S], F32, name="inv_sb")
+        nc.sync.dma_start(inv_sb[:], inv)
+
+        warm_in = keep.tile([P, 1], F32, name="warm_in")
+        warm_exp = keep.tile([P, 1], F32, name="warm_exp")
+        nc.vector.memset(warm_in[:], 0.0)
+        nc.scalar.activation(warm_exp[:], warm_in[:], ACT.Exp)
+
+        w_bf = keep.tile([P, N, PACK], BF16, name="w_bf", tag="stage0", align_bytes=64)
+        nc.scalar.copy(w_bf[:], w_raw[:].rearrange("p j m -> p m j"))
+        picked_scales = keep.tile([P, S], U8, name="picked_scales", align_bytes=64)
+        nc.vector.tensor_copy(picked_scales[:], scale_table[:].indirect(offs_sb[:]))
+        w_codes = keep.tile([P, N], U32, name="w_codes", align_bytes=64)
+        w_scales = keep.tile([P, N], U8, name="w_scales", align_bytes=64)
+        nc.vector.quantize_mx(
+            out=w_codes[:].bitcast(FP8X4),
+            scales=w_scales[:],
+            in_=w_bf[:].rearrange("p m j -> p (m j)"),
+        )
+
+        exp_y = keep.tile([P, S], F32, name="exp_y")
+        y_banks = []
+        for c, (a, b) in enumerate(SAMPLE_CHUNKS):
+            picked_words = keep.tile([P, b - a], U32, name="picked_words%d" % c, tag="stage%d" % c, align_bytes=64)
+            nc.vector.tensor_copy(
+                picked_words[:],
+                word_table[:].bitcast(U32).indirect(offs_sb[:, a // STRIPE : b // STRIPE]),
+            )
+            y = psum.tile([P, b - a], F32, name="y%d" % c)
+            nc.tensor.matmul_mx(
+                out=y[:],
+                lhsT=w_codes[:].bitcast(FP8X4),
+                lhsT_scale=w_scales[:],
+                rhs=picked_words[:].bitcast(FP8X4),
+                rhs_scale=picked_scales[:, a:b],
+                start=True,
+                stop=True,
+            )
+            nc.scalar.activation(exp_y[:, a:b], y[:], ACT.Exp)
+            y_banks.append(y)
+
+        cnt_sum = [keep.tile([P, V], F32, name="cnt_sum%d" % i) for i in range(3)]
+        weight = keep.tile([P, S], F32, name="weight")
+        nc.vector.tensor_copy(cnt_sum[0][:], cnt_sb[:].indirect(pos_sb[0][:]))
+        nc.vector.tensor_tensor(weight[:], inv_sb[:], cnt_sb[:], ALU.mult)
+        for i in (1, 2):
+            nc.vector.tensor_tensor(
+                cnt_sum[i][:], cnt_sb[:].indirect(pos_sb[i][:]), cnt_sum[i - 1][:], ALU.add
+            )
+
+        log1p = keep.tile([P, S], F32, name="log1p")
+        for a, b in ((0, LN_CUT), (LN_CUT, S)):
+            nc.scalar.activation(log1p[:, a:b], exp_y[:, a:b], ACT.Ln, bias=1.0)
+        warm_rsqrt = keep.tile([P, 1], F32, name="warm_rsqrt")
+        nc.scalar.activation(warm_rsqrt[:], log1p[:, S - 1 : S], ACT.Abs_reciprocal_sqrt)
+
+        tgt = keep.tile([P, S], F32, name="tgt")
+        res = keep.tile([P, S], F32, name="res")
+        res_tgt = keep.tile([P, S], F32, name="res_tgt")
+        for (a, b), y in zip(SAMPLE_CHUNKS, y_banks):
+            nc.vector.scalar_tensor_tensor(
+                tgt[:, a:b], log1p[:, a:b], SOFTPLUS_CAP, y[:], ALU.min, ALU.max
+            )
+        for a, b in SAMPLE_CHUNKS:
+            nc.vector.scalar_tensor_tensor(
+                res[:, a:b], tgt[:, a:b], TINY, weight[:, a:b], ALU.max, ALU.mult
+            )
+        for a, b in SAMPLE_CHUNKS:
+            nc.vector.tensor_tensor(res_tgt[:, a:b], res[:, a:b], tgt[:, a:b], ALU.mult)
+
+        for c, (a, b) in enumerate(PIXEL_CHUNKS):
+            n = b - a
+            lists = [pos_tile[:, a // STRIPE : b // STRIPE] for pos_tile in pos_sb]
+            tot = [keep.tile([P, n], F32, name="tot%d_%d" % (c, i)) for i in range(3)]
+            sq = [keep.tile([P, n], F32, name="sq%d_%d" % (c, i)) for i in range(3)]
+            nc.vector.tensor_copy(tot[0][:], res[:].indirect(lists[0]))
+            nc.vector.tensor_copy(sq[0][:], res_tgt[:].indirect(lists[0]))
+            for i in (1, 2):
+                nc.vector.tensor_tensor(sq[i][:], res_tgt[:].indirect(lists[i]), sq[i - 1][:], ALU.add)
+                nc.vector.tensor_tensor(tot[i][:], res[:].indirect(lists[i]), tot[i - 1][:], ALU.add)
+            sq_cnt = keep.tile([P, n], F32, name="sq_cnt%d" % c)
+            den = keep.tile([P, n], F32, name="den%d" % c)
+            nc.vector.tensor_tensor(sq_cnt[:], sq[2][:], cnt_sum[2][:, a:b], ALU.mult)
+            nc.vector.scalar_tensor_tensor(den[:], tot[2][:], 0.5, sq_cnt[:], ALU.mult, ALU.add)
+            sign = keep.tile([P, n], F32, name="sign%d" % c)
+            rsqrt = keep.tile([P, n], F32, name="rsqrt%d" % c)
+            recip = keep.tile([P, n], F32, name="recip%d" % c)
+            nc.scalar.activation(sign[:], den[:], ACT.Sign)
+            nc.scalar.activation(rsqrt[:], den[:], ACT.Abs_reciprocal_sqrt)
+            nc.scalar.activation(recip[:], rsqrt[:], ACT.Square)
+            signed_tot = keep.tile([P, n], F32, name="signed_tot%d" % c)
+            ratio = keep.tile([P, n], F32, name="ratio%d" % c)
+            result = keep.tile([P, n], F32, name="result%d" % c)
+            nc.vector.tensor_tensor(signed_tot[:], tot[2][:], sign[:], ALU.mult)
+            nc.vector.tensor_tensor(ratio[:], signed_tot[:], recip[:], ALU.mult)
+            nc.vector.tensor_tensor(result[:], ratio[:], tot[2][:], ALU.mult)
+            nc.sync.dma_start(out[:, a:b], result[:])

@@ -37,18 +37,19 @@ def tile_picked_yrestir_inv_p_kernel(
         nc.sync.dma_start(offs_sb[:], offs)
 
         scale_table = keep.tile([P, T], U8, name="scale_table", align_bytes=64)
-        nc.vector.memset(scale_table[:].bitcast(I32), 0)
         for q in range(4):
-            nc.scalar.dma_start(
-                scale_table[32 * q : 32 * q + 4, :].bitcast(I32),
-                x_scales[0][4 * q : 4 * q + 4, :].bitcast(I32),
+            queue = nc.sync if q < 2 else nc.scalar
+            rows = x_scales[0][4 * q : 4 * q + 4, :].bitcast(I32)
+            queue.dma_start(
+                scale_table[32 * q : 32 * q + 32, :].bitcast(I32),
+                rows.unsqueeze(0).broadcast_to([8, 4, T // 4]),
             )
 
-        w_raw = keep.tile([P, PACK, N], F32, name="w_raw")
-        nc.sync.dma_start(w_raw[:], w1.rearrange("(p j) m -> p j m", j=PACK))
         word_table = keep.tile([P, T], I32, name="word_table", align_bytes=64)
         nc.sync.dma_start(word_table[:], x_words[0].rearrange("p n t -> p (n t)").bitcast(I32))
-        cnt_sb = keep.tile([P, S], F32, name="cnt_sb")
+        w_raw = keep.tile([P, PACK, N], F32, name="w_raw")
+        nc.sync.dma_start(w_raw[:], w1.rearrange("(p j) m -> p j m", j=PACK))
+        cnt_sb = keep.tile([P, S], F32, name="cnt_sb", tag="cnt_then_tgt")
         nc.sync.dma_start(cnt_sb[:], cnt)
         pos_sb = []
         for i, pos in enumerate((pos1, pos2, pos3)):
@@ -58,15 +59,16 @@ def tile_picked_yrestir_inv_p_kernel(
         inv_sb = keep.tile([P, S], F32, name="inv_sb")
         nc.sync.dma_start(inv_sb[:], inv)
 
-        warm_in = keep.tile([P, 1], F32, name="warm_in")
-        warm_exp = keep.tile([P, 1], F32, name="warm_exp")
-        nc.vector.memset(warm_in[:], 0.0)
-        nc.scalar.activation(warm_exp[:], warm_in[:], ACT.Exp)
-
-        w_bf = keep.tile([P, N, PACK], BF16, name="w_bf", tag="stage0", align_bytes=64)
-        nc.scalar.copy(w_bf[:], w_raw[:].rearrange("p j m -> p m j"))
+        w_bf = keep.tile([P, N, PACK], BF16, name="w_bf", tag="after_quantize", align_bytes=64)
+        nc.scalar.activation(
+            w_bf[:].rearrange("p (c i) j -> p c j i", i=4),
+            w_raw[:].rearrange("p j (c i) -> p c j i", i=4),
+            ACT.Copy,
+        )
         picked_scales = keep.tile([P, S], U8, name="picked_scales", align_bytes=64)
         nc.vector.tensor_copy(picked_scales[:], scale_table[:].indirect(offs_sb[:]))
+        picked_words = keep.tile([P, S], U32, name="picked_words", align_bytes=64)
+        nc.vector.tensor_copy(picked_words[:], word_table[:].bitcast(U32).indirect(offs_sb[:]))
         w_codes = keep.tile([P, N], U32, name="w_codes", align_bytes=64)
         w_scales = keep.tile([P, N], U8, name="w_scales", align_bytes=64)
         nc.vector.quantize_mx(
@@ -78,17 +80,12 @@ def tile_picked_yrestir_inv_p_kernel(
         exp_y = keep.tile([P, S], F32, name="exp_y")
         y_banks = []
         for c, (a, b) in enumerate(SAMPLE_CHUNKS):
-            picked_words = keep.tile([P, b - a], U32, name="picked_words%d" % c, tag="stage%d" % c, align_bytes=64)
-            nc.vector.tensor_copy(
-                picked_words[:],
-                word_table[:].bitcast(U32).indirect(offs_sb[:, a // STRIPE : b // STRIPE]),
-            )
             y = psum.tile([P, b - a], F32, name="y%d" % c)
             nc.tensor.matmul_mx(
                 out=y[:],
                 lhsT=w_codes[:].bitcast(FP8X4),
                 lhsT_scale=w_scales[:],
-                rhs=picked_words[:].bitcast(FP8X4),
+                rhs=picked_words[:, a:b].bitcast(FP8X4),
                 rhs_scale=picked_scales[:, a:b],
                 start=True,
                 stop=True,
@@ -96,59 +93,59 @@ def tile_picked_yrestir_inv_p_kernel(
             nc.scalar.activation(exp_y[:, a:b], y[:], ACT.Exp)
             y_banks.append(y)
 
-        cnt_sum = [keep.tile([P, V], F32, name="cnt_sum%d" % i) for i in range(3)]
-        weight = keep.tile([P, S], F32, name="weight")
+        cnt_sum = [keep.tile([P, V], F32, name="cnt_sum0", tag="after_quantize", align_bytes=64)]
         nc.vector.tensor_copy(cnt_sum[0][:], cnt_sb[:].indirect(pos_sb[0][:]))
-        nc.vector.tensor_tensor(weight[:], inv_sb[:], cnt_sb[:], ALU.mult)
         for i in (1, 2):
+            cnt_sum.append(keep.tile([P, V], F32, name="cnt_sum%d" % i))
             nc.vector.tensor_tensor(
                 cnt_sum[i][:], cnt_sb[:].indirect(pos_sb[i][:]), cnt_sum[i - 1][:], ALU.add
             )
+        weight = keep.tile([P, S], F32, name="weight", tag="after_quantize", align_bytes=64)
+        nc.vector.tensor_tensor(weight[:], inv_sb[:], cnt_sb[:], ALU.mult)
 
         log1p = keep.tile([P, S], F32, name="log1p")
         for a, b in ((0, LN_CUT), (LN_CUT, S)):
             nc.scalar.activation(log1p[:, a:b], exp_y[:, a:b], ACT.Ln, bias=1.0)
-        warm_rsqrt = keep.tile([P, 1], F32, name="warm_rsqrt")
-        nc.scalar.activation(warm_rsqrt[:], log1p[:, S - 1 : S], ACT.Abs_reciprocal_sqrt)
 
-        tgt = keep.tile([P, S], F32, name="tgt")
+        tgt = keep.tile([P, S], F32, name="tgt", tag="cnt_then_tgt")
         res = keep.tile([P, S], F32, name="res")
         res_tgt = keep.tile([P, S], F32, name="res_tgt")
         for (a, b), y in zip(SAMPLE_CHUNKS, y_banks):
             nc.vector.scalar_tensor_tensor(
                 tgt[:, a:b], log1p[:, a:b], SOFTPLUS_CAP, y[:], ALU.min, ALU.max
             )
-        for a, b in SAMPLE_CHUNKS:
+        for a, b in ((0, 256), (256, 512)):
             nc.vector.scalar_tensor_tensor(
                 res[:, a:b], tgt[:, a:b], TINY, weight[:, a:b], ALU.max, ALU.mult
             )
-        for a, b in SAMPLE_CHUNKS:
+        for a, b in ((0, 256), (256, 512)):
             nc.vector.tensor_tensor(res_tgt[:, a:b], res[:, a:b], tgt[:, a:b], ALU.mult)
 
+        tot01 = [keep.tile([P, V], F32, name="tot_part%d" % i) for i in range(2)]
+        sq01 = [keep.tile([P, V], F32, name="sq_part%d" % i) for i in range(2)]
+        nc.vector.tensor_copy(tot01[0][:], res[:].indirect(pos_sb[0][:]))
+        nc.vector.tensor_copy(sq01[0][:], res_tgt[:].indirect(pos_sb[0][:]))
+        nc.vector.tensor_tensor(tot01[1][:], res[:].indirect(pos_sb[1][:]), tot01[0][:], ALU.add)
+        nc.vector.tensor_tensor(sq01[1][:], res_tgt[:].indirect(pos_sb[1][:]), sq01[0][:], ALU.add)
         for c, (a, b) in enumerate(PIXEL_CHUNKS):
             n = b - a
-            lists = [pos_tile[:, a // STRIPE : b // STRIPE] for pos_tile in pos_sb]
-            tot = [keep.tile([P, n], F32, name="tot%d_%d" % (c, i)) for i in range(3)]
-            sq = [keep.tile([P, n], F32, name="sq%d_%d" % (c, i)) for i in range(3)]
-            nc.vector.tensor_copy(tot[0][:], res[:].indirect(lists[0]))
-            nc.vector.tensor_copy(sq[0][:], res_tgt[:].indirect(lists[0]))
-            for i in (1, 2):
-                nc.vector.tensor_tensor(sq[i][:], res_tgt[:].indirect(lists[i]), sq[i - 1][:], ALU.add)
-                nc.vector.tensor_tensor(tot[i][:], res[:].indirect(lists[i]), tot[i - 1][:], ALU.add)
+            last = pos_sb[2][:, a // STRIPE : b // STRIPE]
+            sq = keep.tile([P, n], F32, name="sq%d" % c)
+            tot = keep.tile([P, n], F32, name="tot%d" % c)
+            nc.vector.tensor_tensor(sq[:], res_tgt[:].indirect(last), sq01[1][:, a:b], ALU.add)
+            nc.vector.tensor_tensor(tot[:], res[:].indirect(last), tot01[1][:, a:b], ALU.add)
             sq_cnt = keep.tile([P, n], F32, name="sq_cnt%d" % c)
             den = keep.tile([P, n], F32, name="den%d" % c)
-            nc.vector.tensor_tensor(sq_cnt[:], sq[2][:], cnt_sum[2][:, a:b], ALU.mult)
-            nc.vector.scalar_tensor_tensor(den[:], tot[2][:], 0.5, sq_cnt[:], ALU.mult, ALU.add)
+            nc.vector.tensor_tensor(sq_cnt[:], sq[:], cnt_sum[2][:, a:b], ALU.mult)
+            nc.vector.scalar_tensor_tensor(den[:], tot[:], 0.5, sq_cnt[:], ALU.mult, ALU.add)
             sign = keep.tile([P, n], F32, name="sign%d" % c)
             rsqrt = keep.tile([P, n], F32, name="rsqrt%d" % c)
-            recip = keep.tile([P, n], F32, name="recip%d" % c)
-            nc.scalar.activation(sign[:], den[:], ACT.Sign)
-            nc.scalar.activation(rsqrt[:], den[:], ACT.Abs_reciprocal_sqrt)
-            nc.scalar.activation(recip[:], rsqrt[:], ACT.Square)
-            signed_tot = keep.tile([P, n], F32, name="signed_tot%d" % c)
-            ratio = keep.tile([P, n], F32, name="ratio%d" % c)
+            root = keep.tile([P, n], F32, name="root%d" % c)
+            size = keep.tile([P, n], F32, name="size%d" % c)
             result = keep.tile([P, n], F32, name="result%d" % c)
-            nc.vector.tensor_tensor(signed_tot[:], tot[2][:], sign[:], ALU.mult)
-            nc.vector.tensor_tensor(ratio[:], signed_tot[:], recip[:], ALU.mult)
-            nc.vector.tensor_tensor(result[:], ratio[:], tot[2][:], ALU.mult)
+            nc.scalar.activation(rsqrt[:], den[:], ACT.Abs_reciprocal_sqrt)
+            nc.scalar.activation(sign[:], den[:], ACT.Sign)
+            nc.vector.tensor_tensor(root[:], tot[:], rsqrt[:], ALU.mult)
+            nc.scalar.activation(size[:], root[:], ACT.Square)
+            nc.vector.tensor_tensor(result[:], size[:], sign[:], ALU.mult)
             nc.sync.dma_start(out[:, a:b], result[:])

from contextlib import ExitStack

import concourse.mybir as mybir

K, T, S, N, V = 512, 1024, 512, 128, 256
FLOPS = 2 * K * N * S

F32 = mybir.dt.float32
BF16 = mybir.dt.bfloat16
I32 = mybir.dt.int32
U32 = mybir.dt.uint32
U16 = mybir.dt.uint16
U8 = mybir.dt.uint8
FP8X4 = mybir.dt.float8_e4m3fn_x4
ALU = mybir.AluOpType
ACT = mybir.ActivationFunctionType

P = 128
PACK = 4
STRIPE = 16
SOFTPLUS_CAP = 40.0
TINY = 1e-30
SAMPLE_CHUNKS = ((0, 256), (256, 512))
LN_CUT = 272
PIXEL_CHUNKS = ((0, 128), (128, 256))


def tile_picked_yrestir_inv_p_kernel(
    tc, x_words, x_scales, w1, inv, cnt, offs, pos1, pos2, pos3, out
):
    nc = tc.nc
    with ExitStack() as ctx:
        keep = ctx.enter_context(tc.tile_pool(name="keep", bufs=1))
        psum = ctx.enter_context(tc.psum_pool(name="psum", bufs=1))

        offs_sb = keep.tile([P, S // STRIPE], U16, name="offs_sb")
        nc.sync.dma_start(offs_sb[:], offs)

        scale_table = keep.tile([P, T], U8, name="scale_table", align_bytes=64)
        for q in range(4):
            queue = nc.sync if q < 2 else nc.scalar
            rows = x_scales[0][4 * q : 4 * q + 4, :].bitcast(I32)
            queue.dma_start(
                scale_table[32 * q : 32 * q + 32, :].bitcast(I32),
                rows.unsqueeze(0).broadcast_to([8, 4, T // 4]),
            )

        word_table = keep.tile([P, T], I32, name="word_table", align_bytes=64)
        nc.sync.dma_start(word_table[:], x_words[0].rearrange("p n t -> p (n t)").bitcast(I32))
        w_raw = keep.tile([P, PACK, N], F32, name="w_raw")
        nc.sync.dma_start(w_raw[:], w1.rearrange("(p j) m -> p j m", j=PACK))
        cnt_sb = keep.tile([P, S], F32, name="cnt_sb", tag="cnt_then_tgt")
        nc.sync.dma_start(cnt_sb[:], cnt)
        pos_sb = []
        for i, pos in enumerate((pos1, pos2, pos3)):
            pos_tile = keep.tile([P, V // STRIPE], U16, name="pos_sb%d" % i)
            nc.sync.dma_start(pos_tile[:], pos)
            pos_sb.append(pos_tile)
        inv_sb = keep.tile([P, S], F32, name="inv_sb")
        nc.sync.dma_start(inv_sb[:], inv)

        w_bf = keep.tile([P, N, PACK], BF16, name="w_bf", tag="after_quantize", align_bytes=64)
        nc.scalar.activation(
            w_bf[:].rearrange("p (c i) j -> p c j i", i=4),
            w_raw[:].rearrange("p j (c i) -> p c j i", i=4),
            ACT.Copy,
        )
        picked_scales = keep.tile([P, S], U8, name="picked_scales", align_bytes=64)
        nc.vector.tensor_copy(picked_scales[:], scale_table[:].indirect(offs_sb[:]))
        picked_words = keep.tile([P, S], U32, name="picked_words", align_bytes=64)
        nc.vector.tensor_copy(picked_words[:], word_table[:].bitcast(U32).indirect(offs_sb[:]))
        w_codes = keep.tile([P, N], U32, name="w_codes", align_bytes=64)
        w_scales = keep.tile([P, N], U8, name="w_scales", align_bytes=64)
        nc.vector.quantize_mx(
            out=w_codes[:].bitcast(FP8X4),
            scales=w_scales[:],
            in_=w_bf[:].rearrange("p m j -> p (m j)"),
        )

        exp_y = keep.tile([P, S], F32, name="exp_y")
        y_banks = []
        for c, (a, b) in enumerate(SAMPLE_CHUNKS):
            y = psum.tile([P, b - a], F32, name="y%d" % c)
            nc.tensor.matmul_mx(
                out=y[:],
                lhsT=w_codes[:].bitcast(FP8X4),
                lhsT_scale=w_scales[:],
                rhs=picked_words[:, a:b].bitcast(FP8X4),
                rhs_scale=picked_scales[:, a:b],
                start=True,
                stop=True,
            )
            nc.scalar.activation(exp_y[:, a:b], y[:], ACT.Exp)
            y_banks.append(y)

        cnt_sum = [keep.tile([P, V], F32, name="cnt_sum0", tag="after_quantize", align_bytes=64)]
        nc.vector.tensor_copy(cnt_sum[0][:], cnt_sb[:].indirect(pos_sb[0][:]))
        for i in (1, 2):
            cnt_sum.append(keep.tile([P, V], F32, name="cnt_sum%d" % i))
            nc.vector.tensor_tensor(
                cnt_sum[i][:], cnt_sb[:].indirect(pos_sb[i][:]), cnt_sum[i - 1][:], ALU.add
            )
        weight = keep.tile([P, S], F32, name="weight", tag="after_quantize", align_bytes=64)
        nc.vector.tensor_tensor(weight[:], inv_sb[:], cnt_sb[:], ALU.mult)

        log1p = keep.tile([P, S], F32, name="log1p")
        for a, b in ((0, LN_CUT), (LN_CUT, S)):
            nc.scalar.activation(log1p[:, a:b], exp_y[:, a:b], ACT.Ln, bias=1.0)

        tgt = keep.tile([P, S], F32, name="tgt", tag="cnt_then_tgt")
        res = keep.tile([P, S], F32, name="res")
        res_tgt = keep.tile([P, S], F32, name="res_tgt")
        for (a, b), y in zip(SAMPLE_CHUNKS, y_banks):
            nc.vector.scalar_tensor_tensor(
                tgt[:, a:b], log1p[:, a:b], SOFTPLUS_CAP, y[:], ALU.min, ALU.max
            )
        for a, b in ((0, 256), (256, 512)):
            nc.vector.scalar_tensor_tensor(
                res[:, a:b], tgt[:, a:b], TINY, weight[:, a:b], ALU.max, ALU.mult
            )
        for a, b in ((0, 256), (256, 512)):
            nc.vector.tensor_tensor(res_tgt[:, a:b], res[:, a:b], tgt[:, a:b], ALU.mult)

        tot01 = [keep.tile([P, V], F32, name="tot_part%d" % i) for i in range(2)]
        sq01 = [keep.tile([P, V], F32, name="sq_part%d" % i) for i in range(2)]
        nc.vector.tensor_copy(tot01[0][:], res[:].indirect(pos_sb[0][:]))
        nc.vector.tensor_copy(sq01[0][:], res_tgt[:].indirect(pos_sb[0][:]))
        nc.vector.tensor_tensor(tot01[1][:], res[:].indirect(pos_sb[1][:]), tot01[0][:], ALU.add)
        nc.vector.tensor_tensor(sq01[1][:], res_tgt[:].indirect(pos_sb[1][:]), sq01[0][:], ALU.add)
        for c, (a, b) in enumerate(PIXEL_CHUNKS):
            n = b - a
            last = pos_sb[2][:, a // STRIPE : b // STRIPE]
            sq = keep.tile([P, n], F32, name="sq%d" % c)
            tot = keep.tile([P, n], F32, name="tot%d" % c)
            nc.vector.tensor_tensor(sq[:], res_tgt[:].indirect(last), sq01[1][:, a:b], ALU.add)
            nc.vector.tensor_tensor(tot[:], res[:].indirect(last), tot01[1][:, a:b], ALU.add)
            sq_cnt = keep.tile([P, n], F32, name="sq_cnt%d" % c)
            den = keep.tile([P, n], F32, name="den%d" % c)
            nc.vector.tensor_tensor(sq_cnt[:], sq[:], cnt_sum[2][:, a:b], ALU.mult)
            nc.vector.scalar_tensor_tensor(den[:], tot[:], 0.5, sq_cnt[:], ALU.mult, ALU.add)
            sign = keep.tile([P, n], F32, name="sign%d" % c)
            rsqrt = keep.tile([P, n], F32, name="rsqrt%d" % c)
            root = keep.tile([P, n], F32, name="root%d" % c)
            size = keep.tile([P, n], F32, name="size%d" % c)
            result = keep.tile([P, n], F32, name="result%d" % c)
            nc.scalar.activation(rsqrt[:], den[:], ACT.Abs_reciprocal_sqrt)
            nc.scalar.activation(sign[:], den[:], ACT.Sign)
            nc.vector.tensor_tensor(root[:], tot[:], rsqrt[:], ALU.mult)
            nc.scalar.activation(size[:], root[:], ACT.Square)
            nc.vector.tensor_tensor(result[:], size[:], sign[:], ALU.mult)
            nc.sync.dma_start(out[:, a:b], result[:])
